import numpy as np
import ml_dtypes


def mxq(x, axis, fmt="e4m3"):
    dtype, down = {"e4m3": (ml_dtypes.float8_e4m3fn, 7), "e5m2": (ml_dtypes.float8_e5m2, 14)}[fmt]
    v = np.moveaxis(np.asarray(x, np.float32).astype(ml_dtypes.bfloat16).astype(np.float64), axis, -1)
    blocks = v.reshape(v.shape[:-1] + (-1, 32))
    amax = np.abs(blocks).max(-1, keepdims=True)
    byte = np.maximum(np.where(amax > 0, np.frexp(amax)[1] - 1 + 127, 0) - down, 1)
    scale = np.exp2(byte - 127.0)
    codes = (blocks / scale).astype(np.float32).astype(dtype).astype(np.float64)
    return np.moveaxis((codes * scale).reshape(v.shape), -1, axis)


WIDE = False


def mx_kscale(k):
    if not WIDE:
        return np.ones(k)
    levels = np.array([30, -30])
    if k % 512:
        return np.exp2(np.random.permutation(np.resize(levels, k // 32))).repeat(32)
    a = np.empty((k // 512, 16))
    for p in range(k // 512):
        a[p, :8] = np.random.permutation(np.resize(levels, 8))
        for g in range(8):
            far = levels[np.abs(levels - a[p, g]) >= 10]
            a[p, g + 8] = far[np.random.randint(len(far))]
    return np.exp2(a.ravel()).repeat(32)


def f64(x):
    return np.asarray(x).astype(np.float64)


def striped(idx):
    return np.tile(np.asarray(idx).reshape(-1, 16).T, (8, 1)).astype(np.uint16)


def unstriped(offs):
    return offs[:16].T.reshape(-1).astype(np.int64)


E2M1 = np.array([0.0, 0.5, 1.0, 1.5, 2.0, 3.0, 4.0, 6.0, -0.0, -0.5, -1.0, -1.5, -2.0, -3.0, -4.0, -6.0])


def pack_weight(w, fmt):
    k, n = w.shape
    w = f64(np.asarray(w, np.float32).astype(ml_dtypes.bfloat16)).reshape(k // 32, 32, n)
    amax = np.abs(w).max(1)
    if fmt == "e4m3":
        byte = np.frexp(amax)[1] - 1 + 127 - 7
    else:
        mant, ex = np.frexp(amax / 6.0)
        byte = np.where(mant > 0.5, ex, ex - 1) + 127
    byte = np.clip(np.where(amax > 0, byte, 1), 1, 254)
    scaled = (w * np.exp2(127.0 - byte)[:, None, :]).reshape(k, n).astype(np.float32)
    by_word = np.ascontiguousarray(scaled.reshape(k // 512, 128, 4, n).transpose(0, 1, 3, 2))
    if fmt == "e4m3":
        words = by_word.astype(ml_dtypes.float8_e4m3fn).view(np.uint8)
    else:
        c = by_word.astype(ml_dtypes.float4_e2m1fn).view(np.uint8) & 0xF
        words = (c[..., 0::2] | (c[..., 1::2] << 4)).reshape(k // 512, 128, 2 * n)
    return np.ascontiguousarray(words), np.ascontiguousarray(byte.astype(np.uint8).reshape(k // 512, 16, n))


def unpack_weight(words, scales, fmt):
    g, _, n = scales.shape
    words = np.ascontiguousarray(words).reshape(g, 128, n, -1)
    if fmt == "e4m3":
        vals = words.view(ml_dtypes.float8_e4m3fn).astype(np.float64)
    else:
        nib = np.empty((g, 128, n, 4), np.uint8)
        nib[..., 0::2] = words & 0xF
        nib[..., 1::2] = words >> 4
        vals = E2M1[nib]
    vals = vals * np.repeat(np.exp2(scales.astype(np.float64) - 127.0), 8, axis=1)[..., None]
    return vals.transpose(0, 1, 3, 2).reshape(g * 512, n)


K, T, J, R, V, N = 512, 1024, 256, 512, 512, 256


def setup_inputs():
    n = np.random.standard_normal
    idx = np.random.permutation(T)[:J]
    idx2 = np.random.permutation(T)[:J]
    idx3 = np.random.permutation(V)[:J]
    fk = mx_kscale(K)
    fr = mx_kscale(R)
    wp = pack_weight(n((K, R)) * 1 / np.sqrt(K) * fk[:, None] * fr, "e2m1")
    wbp = pack_weight(n((R, N)) * 1 / np.sqrt(R) / fr[:, None], "e4m3")
    return {
        "xf": (n((K, T))).astype(np.float32),
        "fk": (np.random.uniform(0.5, 2.0, (K, 1)) / fk[:, None]).astype(np.float32),
        "w_words": wp[0],
        "w_scales": wp[1],
        "tb": (n((R, V)) * 0.7 * fr[:, None]).astype(np.float32),
        "wb_words": wbp[0],
        "wb_scales": wbp[1],
        "rs": (n((N, J))).astype(np.float32),
        "gm": (np.random.uniform(0.5, 2.0, (N, 1))).astype(np.float32),
        "offs": striped(idx),
        "offs2": striped(idx2),
        "offs3": striped(idx3),
    }


def reference(xf, fk, w_words, w_scales, tb, wb_words, wb_scales, rs, gm, offs, offs2, offs3):
    idx = unstriped(offs)
    idx2 = unstriped(offs2)
    idx3 = unstriped(offs3)
    wu = unpack_weight(w_words, w_scales, "e2m1")
    wbu = unpack_weight(wb_words, wb_scales, "e4m3")
    u = (f64(xf)[:, idx] - f64(xf)[:, idx2]) * f64(fk)
    uq = mxq(u, 0, "e4m3")
    a = wu.T @ uq
    hid = np.maximum(a, f64(tb)[:, idx3])
    hidq = mxq(hid, 0, "e5m2")
    p = wbu.T @ hidq
    y = f64(gm) * p + f64(rs)
    return y

@@ -1,0 +1,154 @@
+from contextlib import ExitStack
+
+import concourse.mybir as mybir
+
+K, T, J, R, V, N = 512, 1024, 256, 512, 512, 256
+FLOPS = 2 * K * R * J + 2 * R * N * J
+
+F32 = mybir.dt.float32
+BF16 = mybir.dt.bfloat16
+I32 = mybir.dt.int32
+U32 = mybir.dt.uint32
+U16 = mybir.dt.uint16
+U8 = mybir.dt.uint8
+E4M3X4 = mybir.dt.float8_e4m3fn_x4
+E5M2X4 = mybir.dt.float8_e5m2_x4
+E2M1X4 = mybir.dt.float4_e2m1fn_x4
+ALU = mybir.AluOpType
+COPY = mybir.ActivationFunctionType.Copy
+
+P = 128
+PACK = 4
+HALVES = 2
+JH = J // HALVES
+LIST_COLS = J // 16
+QUADS = 4
+
+
+def tile_list_pickgaps_abovetable_residual_kernel(
+    tc, xf, fk, w_words, w_scales, tb, wb_words, wb_scales, rs, gm, offs, offs2, offs3, out
+):
+    nc = tc.nc
+    with ExitStack() as ctx:
+        sb = ctx.enter_context(tc.tile_pool(name="sb", bufs=1))
+        ps = ctx.enter_context(tc.psum_pool(name="ps", bufs=1))
+
+        first = sb.tile([P, LIST_COLS], U16, name="first")
+        second = sb.tile([P, LIST_COLS], U16, name="second")
+        third = sb.tile([P, LIST_COLS], U16, name="third")
+        x_pl = [sb.tile([P, T], F32, name="x_pl%d" % t) for t in range(PACK)]
+        t_pl = [sb.tile([P, V], F32, name="t_pl%d" % t) for t in range(PACK)]
+        w_raw = sb.tile([P, 2 * R], U8, name="w_raw", align_bytes=64)
+        ws_raw = sb.tile([P, R], U8, name="ws_raw", align_bytes=64)
+        w_dealt = sb.tile([P, 2 * R], U8, name="w_dealt", align_bytes=64)
+        ws_dealt = sb.tile([P, R], U8, name="ws_dealt", align_bytes=64)
+        wb_sb = sb.tile([P, 4 * N], U8, name="wb_sb", align_bytes=64)
+        wbs_sb = sb.tile([P, N], U8, name="wbs_sb", align_bytes=64)
+        fk_sb = sb.tile([P, PACK], F32, name="fk_sb")
+        gm_sb = sb.tile([P, N // P, 1], F32, name="gm_sb")
+        rs_sb = sb.tile([P, N // P, J], F32, name="rs_sb")
+
+        xf_pl = xf.rearrange("(p t) c -> t p c", t=PACK)
+        tb_pl = tb.rearrange("(p t) c -> t p c", t=PACK)
+
+        nc.gpsimd.memset(ws_raw[:].bitcast(I32), 0)
+        for q in range(QUADS):
+            nc.gpsimd.dma_start(ws_raw[32 * q : 32 * q + 4, :].bitcast(I32), w_scales[0, 4 * q : 4 * q + 4, :].bitcast(I32))
+        nc.vector.memset(wbs_sb[:].bitcast(I32), 0)
+
+        nc.sync.dma_start(x_pl[0][:], xf_pl[0])
+        nc.sync.dma_start(second[:], offs2)
+        nc.sync.dma_start(first[:], offs)
+        nc.sync.dma_start(w_raw[:].bitcast(I32), w_words[0].bitcast(I32))
+        nc.sync.dma_start(x_pl[1][:], xf_pl[1])
+        nc.sync.dma_start(fk_sb[:], fk.rearrange("(p t) o -> p (t o)", t=PACK))
+        nc.sync.dma_start(x_pl[2][:], xf_pl[2])
+        nc.sync.dma_start(x_pl[3][:], xf_pl[3])
+        nc.sync.dma_start(third[:], offs3)
+        for t in range(PACK):
+            nc.sync.dma_start(t_pl[t][:], tb_pl[t])
+        nc.sync.dma_start(wb_sb[:].bitcast(I32), wb_words[0].rearrange("p n t -> p (n t)").bitcast(I32))
+        for q in range(QUADS):
+            nc.sync.dma_start(wbs_sb[32 * q : 32 * q + 4, :].bitcast(I32), wb_scales[0, 4 * q : 4 * q + 4, :].bitcast(I32))
+        nc.sync.dma_start(rs_sb[:], rs.rearrange("(m p) j -> p m j", p=P))
+        with nc.allow_non_contiguous_dma(reason="one factor a partition and output tile"):
+            nc.gpsimd.dma_start(gm_sb[:], gm.rearrange("(m p) o -> p m o", p=P))
+
+        nc.vector.tensor_copy(
+            w_dealt[:].bitcast(U16).rearrange("p (t q) -> p t q", t=PACK),
+            w_raw[:].bitcast(U16).rearrange("p (q t) -> p t q", t=PACK),
+        )
+        nc.vector.tensor_copy(
+            ws_dealt[:].rearrange("p (t q) -> p t q", t=PACK),
+            ws_raw[:].rearrange("p (q t) -> p t q", t=PACK),
+        )
+
+        u_bf = sb.tile([P, J * PACK], BF16, name="u_bf", align_bytes=64)
+        u_by_plane = u_bf[:].rearrange("p (j t) -> p t j", t=PACK)
+        taken = sb.tile([P, PACK, J], F32, name="taken")
+        gaps = sb.tile([P, PACK, J], F32, name="gaps")
+        floor = sb.tile([P, PACK, J], F32, name="floor")
+
+        def spans(cut):
+            width = J // cut
+            return [(slice(c * width, (c + 1) * width), slice(c * width // 16, (c + 1) * width // 16)) for c in range(cut)]
+
+        for t in range(PACK):
+            for cols, lcols in spans(HALVES if t in (0, PACK - 1) else 1):
+                nc.scalar.activation(taken[:, t, cols], x_pl[t][:].indirect(second[:, lcols]), COPY)
+                nc.vector.tensor_tensor(gaps[:, t, cols], x_pl[t][:].indirect(first[:, lcols]), taken[:, t, cols], ALU.subtract)
+                nc.vector.tensor_scalar(u_by_plane[:, t, cols], gaps[:, t, cols], fk_sb[:, t : t + 1], None, ALU.mult)
+        for t in range(PACK):
+            for cols, lcols in spans(HALVES if t == PACK - 1 else 1):
+                nc.scalar.activation(floor[:, t, cols], t_pl[t][:].indirect(third[:, lcols]), COPY)
+
+        a_ps = []
+        for h in range(HALVES):
+            u_codes = sb.tile([P, JH], U32, name="u_codes%d" % h, align_bytes=64)
+            u_scales = sb.tile([P, JH], U8, name="u_scales%d" % h, align_bytes=64)
+            nc.vector.quantize_mx(u_codes[:].bitcast(E4M3X4), u_scales[:], u_bf[:, h * JH * PACK : (h + 1) * JH * PACK])
+            bank = ps.tile([P, PACK, JH], F32, name="a_ps%d" % h)
+            for t in range(PACK):
+                nc.tensor.matmul_mx(
+                    bank[:, t, :],
+                    lhsT=w_dealt[:, 2 * P * t : 2 * P * (t + 1)].bitcast(E2M1X4),
+                    lhsT_scale=ws_dealt[:, P * t : P * (t + 1)],
+                    rhs=u_codes[:].bitcast(E4M3X4),
+                    rhs_scale=u_scales[:],
+                    start=True,
+                    stop=True,
+                )
+            a_ps.append(bank)
+
+        h_bf = []
+        for h in range(HALVES):
+            hid = sb.tile([P, JH * PACK], BF16, name="hid%d" % h, align_bytes=64)
+            nc.vector.tensor_tensor(
+                hid[:].rearrange("p (c i t) -> p c t i", i=4, t=PACK),
+                a_ps[h][:].rearrange("p t (c i) -> p c t i", i=4),
+                floor[:, :, h * JH : (h + 1) * JH].rearrange("p t (c i) -> p c t i", i=4),
+                ALU.max,
+            )
+            h_bf.append(hid)
+
+        out_v = out.rearrange("(m p) j -> p m j", p=P)
+        for h in range(HALVES):
+            cols = slice(h * JH, (h + 1) * JH)
+            h_codes = sb.tile([P, JH], U32, name="h_codes%d" % h, align_bytes=64)
+            h_scales = sb.tile([P, JH], U8, name="h_scales%d" % h, align_bytes=64)
+            nc.vector.quantize_mx(h_codes[:].bitcast(E5M2X4), h_scales[:], h_bf[h][:])
+            for m in range(N // P):
+                p_ps = ps.tile([P, JH], F32, name="p_ps%d%d" % (h, m))
+                nc.tensor.matmul_mx(
+                    p_ps[:],
+                    lhsT=wb_sb[:, 4 * P * m : 4 * P * (m + 1)].bitcast(E4M3X4),
+                    lhsT_scale=wbs_sb[:, P * m : P * (m + 1)],
+                    rhs=h_codes[:].bitcast(E5M2X4),
+                    rhs_scale=h_scales[:],
+                    start=True,
+                    stop=True,
+                )
+                y = sb.tile([P, JH], F32, name="y%d%d" % (h, m))
+                nc.vector.scalar_tensor_tensor(y[:], p_ps[:], gm_sb[:, m, :], rs_sb[:, m, cols], ALU.mult, ALU.add)
+                queue = nc.sync if m == 0 else nc.scalar
+                queue.dma_start(out_v[:, m, cols], y[:])

@@ -53,26 +53,29 @@ def tile_list_pickgaps_abovetable_residual_kernel(
 
         nc.gpsimd.memset(ws_raw[:].bitcast(I32), 0)
         for q in range(QUADS):
-            nc.gpsimd.dma_start(ws_raw[32 * q : 32 * q + 4, :].bitcast(I32), w_scales[0, 4 * q : 4 * q + 4, :].bitcast(I32))
-        nc.vector.memset(wbs_sb[:].bitcast(I32), 0)
+            nc.gpsimd.dma_start(wbs_sb[32 * q : 32 * q + 4, :].bitcast(I32), wb_scales[0, 4 * q : 4 * q + 4, :].bitcast(I32))
+        warm_in = sb.tile([P, 1], F32, name="warm_in")
+        warm_out = sb.tile([P, 1], F32, name="warm_out")
+        nc.vector.memset(warm_in[:], 0.0)
+        nc.scalar.activation(warm_out[:], warm_in[:], COPY)
 
-        nc.sync.dma_start(x_pl[0][:], xf_pl[0])
         nc.sync.dma_start(second[:], offs2)
-        nc.sync.dma_start(first[:], offs)
         nc.sync.dma_start(w_raw[:].bitcast(I32), w_words[0].bitcast(I32))
+        nc.sync.dma_start(x_pl[0][:], xf_pl[0])
+        for q in range(QUADS):
+            nc.sync.dma_start(ws_raw[32 * q : 32 * q + 4, :].bitcast(I32), w_scales[0, 4 * q : 4 * q + 4, :].bitcast(I32))
         nc.sync.dma_start(x_pl[1][:], xf_pl[1])
-        nc.sync.dma_start(fk_sb[:], fk.rearrange("(p t) o -> p (t o)", t=PACK))
+        nc.sync.dma_start(first[:], offs)
         nc.sync.dma_start(x_pl[2][:], xf_pl[2])
+        nc.sync.dma_start(fk_sb[:], fk.rearrange("(p t) o -> p (t o)", t=PACK))
         nc.sync.dma_start(x_pl[3][:], xf_pl[3])
         nc.sync.dma_start(third[:], offs3)
         for t in range(PACK):
             nc.sync.dma_start(t_pl[t][:], tb_pl[t])
         nc.sync.dma_start(wb_sb[:].bitcast(I32), wb_words[0].rearrange("p n t -> p (n t)").bitcast(I32))
-        for q in range(QUADS):
-            nc.sync.dma_start(wbs_sb[32 * q : 32 * q + 4, :].bitcast(I32), wb_scales[0, 4 * q : 4 * q + 4, :].bitcast(I32))
-        nc.sync.dma_start(rs_sb[:], rs.rearrange("(m p) j -> p m j", p=P))
         with nc.allow_non_contiguous_dma(reason="one factor a partition and output tile"):
-            nc.gpsimd.dma_start(gm_sb[:], gm.rearrange("(m p) o -> p m o", p=P))
+            nc.sync.dma_start(gm_sb[:], gm.rearrange("(m p) o -> p m o", p=P))
+        nc.sync.dma_start(rs_sb[:], rs.rearrange("(m p) j -> p m j", p=P))
 
         nc.vector.tensor_copy(
             w_dealt[:].bitcast(U16).rearrange("p (t q) -> p t q", t=PACK),
@@ -98,8 +101,8 @@ def tile_list_pickgaps_abovetable_residual_kernel(
                 nc.scalar.activation(taken[:, t, cols], x_pl[t][:].indirect(second[:, lcols]), COPY)
                 nc.vector.tensor_tensor(gaps[:, t, cols], x_pl[t][:].indirect(first[:, lcols]), taken[:, t, cols], ALU.subtract)
                 nc.vector.tensor_scalar(u_by_plane[:, t, cols], gaps[:, t, cols], fk_sb[:, t : t + 1], None, ALU.mult)
-        for t in range(PACK):
-            for cols, lcols in spans(HALVES if t == PACK - 1 else 1):
+        for cols, lcols in spans(HALVES):
+            for t in range(PACK):
                 nc.scalar.activation(floor[:, t, cols], t_pl[t][:].indirect(third[:, lcols]), COPY)
 
         a_ps = []
@@ -124,9 +127,9 @@ def tile_list_pickgaps_abovetable_residual_kernel(
         for h in range(HALVES):
             hid = sb.tile([P, JH * PACK], BF16, name="hid%d" % h, align_bytes=64)
             nc.vector.tensor_tensor(
-                hid[:].rearrange("p (c i t) -> p c t i", i=4, t=PACK),
-                a_ps[h][:].rearrange("p t (c i) -> p c t i", i=4),
-                floor[:, :, h * JH : (h + 1) * JH].rearrange("p t (c i) -> p c t i", i=4),
+                hid[:].rearrange("p (c i t) -> p c t i", i=2, t=PACK),
+                a_ps[h][:].rearrange("p t (c i) -> p c t i", i=2),
+                floor[:, :, h * JH : (h + 1) * JH].rearrange("p t (c i) -> p c t i", i=2),
                 ALU.max,
             )
             h_bf.append(hid)

@@ -52,8 +52,6 @@ def tile_list_pickgaps_abovetable_residual_kernel(
         tb_pl = tb.rearrange("(p t) c -> t p c", t=PACK)
 
         nc.gpsimd.memset(ws_raw[:].bitcast(I32), 0)
-        for q in range(QUADS):
-            nc.gpsimd.dma_start(wbs_sb[32 * q : 32 * q + 4, :].bitcast(I32), wb_scales[0, 4 * q : 4 * q + 4, :].bitcast(I32))
         warm_in = sb.tile([P, 1], F32, name="warm_in")
         warm_out = sb.tile([P, 1], F32, name="warm_out")
         nc.vector.memset(warm_in[:], 0.0)
@@ -76,6 +74,8 @@ def tile_list_pickgaps_abovetable_residual_kernel(
         with nc.allow_non_contiguous_dma(reason="one factor a partition and output tile"):
             nc.sync.dma_start(gm_sb[:], gm.rearrange("(m p) o -> p m o", p=P))
         nc.sync.dma_start(rs_sb[:], rs.rearrange("(m p) j -> p m j", p=P))
+        for q in range(QUADS):
+            nc.sync.dma_start(wbs_sb[32 * q : 32 * q + 4, :].bitcast(I32), wb_scales[0, 4 * q : 4 * q + 4, :].bitcast(I32))
 
         nc.vector.tensor_copy(
             w_dealt[:].bitcast(U16).rearrange("p (t q) -> p t q", t=PACK),
@@ -86,9 +86,8 @@ def tile_list_pickgaps_abovetable_residual_kernel(
             ws_raw[:].rearrange("p (q t) -> p t q", t=PACK),
         )
 
-        u_bf = sb.tile([P, J * PACK], BF16, name="u_bf", align_bytes=64)
-        u_by_plane = u_bf[:].rearrange("p (j t) -> p t j", t=PACK)
         taken = sb.tile([P, PACK, J], F32, name="taken")
+        u_planes = sb.tile([P, PACK, J], BF16, name="u_planes")
         gaps = sb.tile([P, PACK, J], F32, name="gaps")
         floor = sb.tile([P, PACK, J], F32, name="floor")
 
@@ -97,19 +96,30 @@ def tile_list_pickgaps_abovetable_residual_kernel(
             return [(slice(c * width, (c + 1) * width), slice(c * width // 16, (c + 1) * width // 16)) for c in range(cut)]
 
         for t in range(PACK):
-            for cols, lcols in spans(HALVES if t in (0, PACK - 1) else 1):
+            pieces = spans(HALVES if t >= 2 else 1)
+            for cols, lcols in pieces:
                 nc.scalar.activation(taken[:, t, cols], x_pl[t][:].indirect(second[:, lcols]), COPY)
                 nc.vector.tensor_tensor(gaps[:, t, cols], x_pl[t][:].indirect(first[:, lcols]), taken[:, t, cols], ALU.subtract)
-                nc.vector.tensor_scalar(u_by_plane[:, t, cols], gaps[:, t, cols], fk_sb[:, t : t + 1], None, ALU.mult)
+            for cols, lcols in pieces:
+                nc.vector.tensor_scalar(u_planes[:, t, cols], gaps[:, t, cols], fk_sb[:, t : t + 1], None, ALU.mult)
+        for t in range(2):
+            nc.scalar.activation(floor[:, t, :], t_pl[t][:].indirect(third[:]), COPY)
         for cols, lcols in spans(HALVES):
-            for t in range(PACK):
+            for t in range(2, PACK):
                 nc.scalar.activation(floor[:, t, cols], t_pl[t][:].indirect(third[:, lcols]), COPY)
 
         a_ps = []
         for h in range(HALVES):
+            u_half = sb.tile([P, JH * PACK], BF16, name="u_half%d" % h, align_bytes=64)
+            width = JH // (h + 1)
+            for c0 in range(0, JH, width):
+                nc.vector.tensor_copy(
+                    u_half[:, c0 * PACK : (c0 + width) * PACK].rearrange("p (c i t) -> p c t i", i=4, t=PACK),
+                    u_planes[:, :, h * JH + c0 : h * JH + c0 + width].rearrange("p t (c i) -> p c t i", i=4),
+                )
             u_codes = sb.tile([P, JH], U32, name="u_codes%d" % h, align_bytes=64)
             u_scales = sb.tile([P, JH], U8, name="u_scales%d" % h, align_bytes=64)
-            nc.vector.quantize_mx(u_codes[:].bitcast(E4M3X4), u_scales[:], u_bf[:, h * JH * PACK : (h + 1) * JH * PACK])
+            nc.vector.quantize_mx(u_codes[:].bitcast(E4M3X4), u_scales[:], u_half[:])
             bank = ps.tile([P, PACK, JH], F32, name="a_ps%d" % h)
             for t in range(PACK):
                 nc.tensor.matmul_mx(

from contextlib import ExitStack

import concourse.mybir as mybir

K, T, J, R, V, N = 512, 1024, 256, 512, 512, 256
FLOPS = 2 * K * R * J + 2 * R * N * J

F32 = mybir.dt.float32
BF16 = mybir.dt.bfloat16
I32 = mybir.dt.int32
U32 = mybir.dt.uint32
U16 = mybir.dt.uint16
U8 = mybir.dt.uint8
E4M3X4 = mybir.dt.float8_e4m3fn_x4
E5M2X4 = mybir.dt.float8_e5m2_x4
E2M1X4 = mybir.dt.float4_e2m1fn_x4
ALU = mybir.AluOpType
COPY = mybir.ActivationFunctionType.Copy

P = 128
PACK = 4
HALVES = 2
JH = J // HALVES
LIST_COLS = J // 16
QUADS = 4


def tile_list_pickgaps_abovetable_residual_kernel(
    tc, xf, fk, w_words, w_scales, tb, wb_words, wb_scales, rs, gm, offs, offs2, offs3, out
):
    nc = tc.nc
    with ExitStack() as ctx:
        sb = ctx.enter_context(tc.tile_pool(name="sb", bufs=1))
        ps = ctx.enter_context(tc.psum_pool(name="ps", bufs=1))

        first = sb.tile([P, LIST_COLS], U16, name="first")
        second = sb.tile([P, LIST_COLS], U16, name="second")
        third = sb.tile([P, LIST_COLS], U16, name="third")
        x_pl = [sb.tile([P, T], F32, name="x_pl%d" % t) for t in range(PACK)]
        t_pl = [sb.tile([P, V], F32, name="t_pl%d" % t) for t in range(PACK)]
        w_raw = sb.tile([P, 2 * R], U8, name="w_raw", align_bytes=64)
        ws_raw = sb.tile([P, R], U8, name="ws_raw", align_bytes=64)
        w_dealt = sb.tile([P, 2 * R], U8, name="w_dealt", align_bytes=64)
        ws_dealt = sb.tile([P, R], U8, name="ws_dealt", align_bytes=64)
        wb_sb = sb.tile([P, 4 * N], U8, name="wb_sb", align_bytes=64)
        wbs_sb = sb.tile([P, N], U8, name="wbs_sb", align_bytes=64)
        fk_sb = sb.tile([P, PACK], F32, name="fk_sb")
        gm_sb = sb.tile([P, N // P, 1], F32, name="gm_sb")
        rs_sb = sb.tile([P, N // P, J], F32, name="rs_sb")

        xf_pl = xf.rearrange("(p t) c -> t p c", t=PACK)
        tb_pl = tb.rearrange("(p t) c -> t p c", t=PACK)

        nc.gpsimd.memset(ws_raw[:].bitcast(I32), 0)
        warm_in = sb.tile([P, 1], F32, name="warm_in")
        warm_out = sb.tile([P, 1], F32, name="warm_out")
        nc.vector.memset(warm_in[:], 0.0)
        nc.scalar.activation(warm_out[:], warm_in[:], COPY)

        nc.sync.dma_start(second[:], offs2)
        nc.sync.dma_start(w_raw[:].bitcast(I32), w_words[0].bitcast(I32))
        nc.sync.dma_start(x_pl[0][:], xf_pl[0])
        for q in range(QUADS):
            nc.sync.dma_start(ws_raw[32 * q : 32 * q + 4, :].bitcast(I32), w_scales[0, 4 * q : 4 * q + 4, :].bitcast(I32))
        nc.sync.dma_start(x_pl[1][:], xf_pl[1])
        nc.sync.dma_start(first[:], offs)
        nc.sync.dma_start(x_pl[2][:], xf_pl[2])
        nc.sync.dma_start(fk_sb[:], fk.rearrange("(p t) o -> p (t o)", t=PACK))
        nc.sync.dma_start(x_pl[3][:], xf_pl[3])
        nc.sync.dma_start(third[:], offs3)
        for t in range(PACK):
            nc.sync.dma_start(t_pl[t][:], tb_pl[t])
        nc.sync.dma_start(wb_sb[:].bitcast(I32), wb_words[0].rearrange("p n t -> p (n t)").bitcast(I32))
        with nc.allow_non_contiguous_dma(reason="one factor a partition and output tile"):
            nc.sync.dma_start(gm_sb[:], gm.rearrange("(m p) o -> p m o", p=P))
        nc.sync.dma_start(rs_sb[:], rs.rearrange("(m p) j -> p m j", p=P))
        for q in range(QUADS):
            nc.sync.dma_start(wbs_sb[32 * q : 32 * q + 4, :].bitcast(I32), wb_scales[0, 4 * q : 4 * q + 4, :].bitcast(I32))

        nc.vector.tensor_copy(
            w_dealt[:].bitcast(U16).rearrange("p (t q) -> p t q", t=PACK),
            w_raw[:].bitcast(U16).rearrange("p (q t) -> p t q", t=PACK),
        )
        nc.vector.tensor_copy(
            ws_dealt[:].rearrange("p (t q) -> p t q", t=PACK),
            ws_raw[:].rearrange("p (q t) -> p t q", t=PACK),
        )

        taken = sb.tile([P, PACK, J], F32, name="taken")
        u_planes = sb.tile([P, PACK, J], BF16, name="u_planes")
        gaps = sb.tile([P, PACK, J], F32, name="gaps")
        floor = sb.tile([P, PACK, J], F32, name="floor")

        def spans(cut):
            width = J // cut
            return [(slice(c * width, (c + 1) * width), slice(c * width // 16, (c + 1) * width // 16)) for c in range(cut)]

        for t in range(PACK):
            pieces = spans(HALVES if t >= 2 else 1)
            for cols, lcols in pieces:
                nc.scalar.activation(taken[:, t, cols], x_pl[t][:].indirect(second[:, lcols]), COPY)
                nc.vector.tensor_tensor(gaps[:, t, cols], x_pl[t][:].indirect(first[:, lcols]), taken[:, t, cols], ALU.subtract)
            for cols, lcols in pieces:
                nc.vector.tensor_scalar(u_planes[:, t, cols], gaps[:, t, cols], fk_sb[:, t : t + 1], None, ALU.mult)
        for t in range(2):
            nc.scalar.activation(floor[:, t, :], t_pl[t][:].indirect(third[:]), COPY)
        for cols, lcols in spans(HALVES):
            for t in range(2, PACK):
                nc.scalar.activation(floor[:, t, cols], t_pl[t][:].indirect(third[:, lcols]), COPY)

        a_ps = []
        for h in range(HALVES):
            u_half = sb.tile([P, JH * PACK], BF16, name="u_half%d" % h, align_bytes=64)
            width = JH // (h + 1)
            for c0 in range(0, JH, width):
                nc.vector.tensor_copy(
                    u_half[:, c0 * PACK : (c0 + width) * PACK].rearrange("p (c i t) -> p c t i", i=4, t=PACK),
                    u_planes[:, :, h * JH + c0 : h * JH + c0 + width].rearrange("p t (c i) -> p c t i", i=4),
                )
            u_codes = sb.tile([P, JH], U32, name="u_codes%d" % h, align_bytes=64)
            u_scales = sb.tile([P, JH], U8, name="u_scales%d" % h, align_bytes=64)
            nc.vector.quantize_mx(u_codes[:].bitcast(E4M3X4), u_scales[:], u_half[:])
            bank = ps.tile([P, PACK, JH], F32, name="a_ps%d" % h)
            for t in range(PACK):
                nc.tensor.matmul_mx(
                    bank[:, t, :],
                    lhsT=w_dealt[:, 2 * P * t : 2 * P * (t + 1)].bitcast(E2M1X4),
                    lhsT_scale=ws_dealt[:, P * t : P * (t + 1)],
                    rhs=u_codes[:].bitcast(E4M3X4),
                    rhs_scale=u_scales[:],
                    start=True,
                    stop=True,
                )
            a_ps.append(bank)

        h_bf = []
        for h in range(HALVES):
            hid = sb.tile([P, JH * PACK], BF16, name="hid%d" % h, align_bytes=64)
            nc.vector.tensor_tensor(
                hid[:].rearrange("p (c i t) -> p c t i", i=2, t=PACK),
                a_ps[h][:].rearrange("p t (c i) -> p c t i", i=2),
                floor[:, :, h * JH : (h + 1) * JH].rearrange("p t (c i) -> p c t i", i=2),
                ALU.max,
            )
            h_bf.append(hid)

        out_v = out.rearrange("(m p) j -> p m j", p=P)
        for h in range(HALVES):
            cols = slice(h * JH, (h + 1) * JH)
            h_codes = sb.tile([P, JH], U32, name="h_codes%d" % h, align_bytes=64)
            h_scales = sb.tile([P, JH], U8, name="h_scales%d" % h, align_bytes=64)
            nc.vector.quantize_mx(h_codes[:].bitcast(E5M2X4), h_scales[:], h_bf[h][:])
            for m in range(N // P):
                p_ps = ps.tile([P, JH], F32, name="p_ps%d%d" % (h, m))
                nc.tensor.matmul_mx(
                    p_ps[:],
                    lhsT=wb_sb[:, 4 * P * m : 4 * P * (m + 1)].bitcast(E4M3X4),
                    lhsT_scale=wbs_sb[:, P * m : P * (m + 1)],
                    rhs=h_codes[:].bitcast(E5M2X4),
                    rhs_scale=h_scales[:],
                    start=True,
                    stop=True,
                )
                y = sb.tile([P, JH], F32, name="y%d%d" % (h, m))
                nc.vector.scalar_tensor_tensor(y[:], p_ps[:], gm_sb[:, m, :], rs_sb[:, m, cols], ALU.mult, ALU.add)
                queue = nc.sync if m == 0 else nc.scalar
                queue.dma_start(out_v[:, m, cols], y[:])
